import numpy as np
import ml_dtypes


def mxq(x, axis, fmt="e4m3"):
    dtype, down = {"e4m3": (ml_dtypes.float8_e4m3fn, 7), "e5m2": (ml_dtypes.float8_e5m2, 14)}[fmt]
    v = np.moveaxis(np.asarray(x, np.float32).astype(ml_dtypes.bfloat16).astype(np.float64), axis, -1)
    blocks = v.reshape(v.shape[:-1] + (-1, 32))
    amax = np.abs(blocks).max(-1, keepdims=True)
    byte = np.maximum(np.where(amax > 0, np.frexp(amax)[1] - 1 + 127, 0) - down, 1)
    scale = np.exp2(byte - 127.0)
    codes = (blocks / scale).astype(np.float32).astype(dtype).astype(np.float64)
    return np.moveaxis((codes * scale).reshape(v.shape), -1, axis)


WIDE = False


def mx_kscale(k):
    if not WIDE:
        return np.ones(k)
    levels = np.array([30, -30])
    if k % 512:
        return np.exp2(np.random.permutation(np.resize(levels, k // 32))).repeat(32)
    a = np.empty((k // 512, 16))
    for p in range(k // 512):
        a[p, :8] = np.random.permutation(np.resize(levels, 8))
        for g in range(8):
            far = levels[np.abs(levels - a[p, g]) >= 10]
            a[p, g + 8] = far[np.random.randint(len(far))]
    return np.exp2(a.ravel()).repeat(32)


BF16 = ml_dtypes.bfloat16


def bf(x):
    return np.asarray(x, np.float32).astype(BF16)


def f64(x):
    return np.asarray(x).astype(np.float64)


E2M1 = np.array([0.0, 0.5, 1.0, 1.5, 2.0, 3.0, 4.0, 6.0, -0.0, -0.5, -1.0, -1.5, -2.0, -3.0, -4.0, -6.0])


def pack_weight(w, fmt):
    k, n = w.shape
    w = f64(bf(w)).reshape(k // 32, 32, n)
    amax = np.abs(w).max(1)
    if fmt in ("e4m3", "e5m2"):
        byte = np.frexp(amax)[1] - 1 + 127 - (7 if fmt == "e4m3" else 14)
    else:
        mant, ex = np.frexp(amax / 6.0)
        byte = np.where(mant > 0.5, ex, ex - 1) + 127
    byte = np.clip(np.where(amax > 0, byte, 1), 1, 254)
    scaled = (w * np.exp2(127.0 - byte)[:, None, :]).reshape(k, n).astype(np.float32)
    by_word = np.ascontiguousarray(scaled.reshape(k // 512, 128, 4, n).transpose(0, 1, 3, 2))
    if fmt in ("e4m3", "e5m2"):
        words = by_word.astype(ml_dtypes.float8_e4m3fn if fmt == "e4m3" else ml_dtypes.float8_e5m2).view(np.uint8)
    else:
        c = by_word.astype(ml_dtypes.float4_e2m1fn).view(np.uint8) & 0xF
        words = c[..., 0::2] | (c[..., 1::2] << 4)
    return np.ascontiguousarray(words), np.ascontiguousarray(byte.astype(np.uint8).reshape(k // 512, 16, n))


def unpack_weight(words, scales, fmt):
    g, p, n, _ = words.shape
    if fmt in ("e4m3", "e5m2"):
        vals = np.ascontiguousarray(words).view(ml_dtypes.float8_e4m3fn if fmt == "e4m3" else ml_dtypes.float8_e5m2).astype(np.float64)
    else:
        nib = np.empty((g, p, n, 4), np.uint8)
        nib[..., 0::2] = words & 0xF
        nib[..., 1::2] = words >> 4
        vals = E2M1[nib]
    vals = vals * np.repeat(np.exp2(scales.astype(np.float64) - 127.0), 8, axis=1)[..., None]
    return vals.transpose(0, 1, 3, 2).reshape(g * 512, n)

def planes(Y):
    n, m = Y.shape
    b = f64(bf(Y)).reshape(n // 32, 32, m)
    amax = np.abs(b).max(1)
    byte = np.clip(np.where(amax > 0, np.frexp(amax)[1] - 1 + 127 - 7, 1), 1, 254)
    codes = (b * np.exp2(127.0 - byte)[:, None, :]).reshape(n, m).astype(np.float32).astype(ml_dtypes.float8_e4m3fn).view(np.uint8)
    words = codes.reshape(n // 512, 128, 4, m).transpose(0, 1, 3, 2)
    return np.ascontiguousarray(words), np.ascontiguousarray(byte.astype(np.uint8).reshape(n // 512, 16, m))


H, T, S, D = 8, 256, 1536, 512
MAP_STD = 2.0
VALUE_STD = 3.0


def setup_inputs():
    s = mx_kscale(S)
    e1 = np.exp(MAP_STD * np.random.randn(S, H * T))
    e2 = np.exp(MAP_STD * np.random.randn(S, H * T))
    a1 = e1 / e1.sum(axis=0, keepdims=True)
    a2 = e2 / e2.sum(axis=0, keepdims=True)
    a1_words, a1_scales = pack_weight(a1 * s[:, None], "e5m2")
    a2_words, a2_scales = pack_weight(a2 * s[:, None], "e5m2")
    c = bf(VALUE_STD * np.random.randn(S, D) / s[:, None])
    lam_logit = bf(np.random.randn(H, T))
    gain = bf(np.exp(0.8 * np.random.randn(H, D)))
    return {"a1_words": a1_words, "a1_scales": a1_scales,
            "a2_words": a2_words, "a2_scales": a2_scales,
            "c": c, "lam_logit": lam_logit, "gain": gain}


def reference(a1_words, a1_scales, a2_words, a2_scales, c, lam_logit, gain):
    A1 = unpack_weight(a1_words, a1_scales, "e5m2")
    A2 = unpack_weight(a2_words, a2_scales, "e5m2")
    Cq = mxq(f64(c), 0, "e4m3")
    R1 = (A1.T @ Cq).reshape(H, T, D)
    R2 = (A2.T @ Cq).reshape(H, T, D)
    lam = 1.0 / (1.0 + np.exp(-f64(lam_logit)))
    y = (R1 - lam[:, :, None] * R2) * f64(gain)[:, None, :]
    Y = y.reshape(H * T, D).T
    words, scales = planes(Y)
    return y, words, scales

@@ -1,0 +1,291 @@
+from contextlib import ExitStack
+
+import concourse.mybir as mybir
+from concourse.masks import make_identity
+
+H, T, S, D = 8, 256, 1536, 512
+M = H * T
+FLOPS = 2 * 2 * M * S * D
+
+F32 = mybir.dt.float32
+BF16 = mybir.dt.bfloat16
+I32 = mybir.dt.int32
+U32 = mybir.dt.uint32
+U8 = mybir.dt.uint8
+E4M3 = mybir.dt.float8_e4m3fn_x4
+E5M2 = mybir.dt.float8_e5m2_x4
+ACT = mybir.ActivationFunctionType
+ALU = mybir.AluOpType
+
+P = 128
+PACK = 4
+PASSES = S // (P * PACK)
+TILES = M // P
+HEAD_TILES = 4
+SCALAR_COLS = 160
+SCALE_RUNS = [(0, 4), (4, 8), (8, 16)]
+WORD_LOADS = [(4, 6), (6, 8), (8, 12), (12, 16)]
+
+
+def tile_differential_latent_read_k2_kernel(
+    tc, a1_words, a1_scales, a2_words, a2_scales, c, lam_logit, gain, out_0, out_1, out_2
+):
+    nc = tc.nc
+    with ExitStack() as ctx:
+        keep = ctx.enter_context(tc.tile_pool(name="keep", bufs=1))
+        work = ctx.enter_context(tc.tile_pool(name="work", bufs=4))
+        psum = ctx.enter_context(tc.psum_pool(name="psum", bufs=1))
+        ctx.enter_context(tc.manual_schedule())
+
+        bank = [psum.tile([P, 512], F32, name="bank%d" % b) for b in range(8)]
+
+        words_hbm = [w.rearrange("g p n t -> p g (n t)").bitcast(I32) for w in (a2_words, a1_words)]
+        scales_hbm = [s.bitcast(I32).rearrange("g (q r) n -> r q g n", r=4) for s in (a2_scales, a1_scales)]
+        a_words = [keep.tile([P, PASSES, M], U32, name="a_words%d" % a, align_bytes=64) for a in range(2)]
+        a_plane = [
+            [
+                keep.tile([P, PASSES, (hi - lo) * P], U8, name="a_plane%d_%d" % (a, lo), align_bytes=64)
+                for lo, hi in SCALE_RUNS
+            ]
+            for a in range(2)
+        ]
+        c_raw = keep.tile([P, PASSES, PACK, D], BF16, align_bytes=64)
+        c_grouped = keep.tile([P, PASSES, D, PACK], BF16, align_bytes=64)
+        c_words = keep.tile([P, PASSES, D], U32, align_bytes=64)
+        c_plane = keep.tile([P, PASSES, D], U8, align_bytes=64)
+        ident = keep.tile([P, P], F32, align_bytes=64)
+        gain_rows = keep.tile([P, 2 * P], BF16, align_bytes=64)
+        gain_cols = keep.tile([P, TILES], F32, align_bytes=64)
+        gain_all = keep.tile([P, H * D], BF16, align_bytes=64)
+        logit_rows = keep.tile([TILES, P], BF16, align_bytes=64)
+        lam_rows = keep.tile([P, P], F32, align_bytes=64)
+        lam = keep.tile([P, TILES], F32, align_bytes=64)
+        y = keep.tile([P, TILES, D], F32, align_bytes=64)
+        y_bf = keep.tile([P, TILES, D], BF16, align_bytes=64)
+        y_grouped = keep.tile([P, TILES, D], BF16, align_bytes=64)
+        y_words = keep.tile([P, M], U32, align_bytes=64)
+        y_plane = keep.tile([P, M], U8, align_bytes=64)
+
+        out_rows = out_0.rearrange("h (a p) d -> p (h a) d", p=P)
+        out_words = out_1.rearrange("g p m t -> p (g m t)").bitcast(I32)
+        out_scales = out_2.rearrange("g q m -> q (g m)").bitcast(I32)
+
+        def load_c(g):
+            rows = c[g * P * PACK : (g + 1) * P * PACK, :]
+            nc.sync.dma_start(out=c_raw[:, g], in_=rows.rearrange("(p j) d -> p j d", j=PACK))
+
+        def load_scales(a, run):
+            lo, hi = SCALE_RUNS[run]
+            plane = a_plane[a][run][:].bitcast(I32)
+            for r in range(4):
+                nc.sync.dma_start(out=plane[r:P:32], in_=scales_hbm[a][r][:, :, lo * P // 4 : hi * P // 4])
+
+        def load_words(a, passes, lo, hi):
+            cols = slice(lo * P, hi * P)
+            nc.sync.dma_start(out=a_words[a][:, passes, cols].bitcast(I32), in_=words_hbm[a][:, passes, cols])
+
+        def clear_plane(a, run):
+            nc.vector.memset(a_plane[a][run][:].rearrange("p g n -> p (g n)").bitcast(I32), 0)
+
+        def interleave(engine_copy, g, lo, hi):
+            engine_copy(out=c_grouped[:, g, lo:hi, :], in_=c_raw[:, g, :, lo:hi].rearrange("p j d -> p d j"))
+
+        def quantize_c(g):
+            nc.vector.quantize_mx(
+                out=c_words[:, g].bitcast(E4M3),
+                scales=c_plane[:, g],
+                in_=c_grouped[:, g].rearrange("p d j -> p (d j)"),
+            )
+
+        def product_bank(a, j):
+            return bank[4 * a + (j if j < HEAD_TILES else (j - HEAD_TILES) % (2 + a))]
+
+        def product_pass(a, j, g):
+            run = [r for r, (lo, hi) in enumerate(SCALE_RUNS) if lo <= j < hi][0]
+            first = (j - SCALE_RUNS[run][0]) * P
+            nc.tensor.matmul_mx(
+                out=product_bank(a, j)[:],
+                lhsT=a_words[a][:, g, j * P : (j + 1) * P].bitcast(E5M2),
+                lhsT_scale=a_plane[a][run][:, g, first : first + P],
+                rhs=c_words[:, g].bitcast(E4M3),
+                rhs_scale=c_plane[:, g],
+                start=(g == 0),
+                stop=(g == PASSES - 1),
+            )
+
+        scaled = {}
+        diff = {}
+
+        def scale_second(j):
+            scaled[j] = work.tile([P, D], F32, name="scaled")
+            nc.scalar.activation(out=scaled[j][:], in_=product_bank(0, j)[:], func=ACT.Copy, scale=lam[:, j : j + 1])
+
+        def subtract(j, cols):
+            if j not in diff:
+                diff[j] = work.tile([P, D], F32, name="diff")
+            nc.vector.tensor_tensor(
+                out=diff[j][:, cols], in0=product_bank(1, j)[:, cols], in1=scaled[j][:, cols], op=ALU.subtract
+            )
+
+        def apply_gain(j, cols):
+            head_gain = gain_all[:, (j // 2) * D : (j // 2 + 1) * D]
+            nc.vector.tensor_tensor(out=y[:, j, cols], in0=diff[j][:, cols], in1=head_gain[:, cols], op=ALU.mult)
+
+        def round_y(engine_copy, j, lo, hi):
+            engine_copy(
+                out=y_bf[:, j].rearrange("m (u p e) -> m u p e", u=2, e=2)[:, :, lo:hi, :],
+                in_=y[:, j].rearrange("m (p u e) -> m u p e", u=2, e=2)[:, :, lo:hi, :],
+            )
+
+        def turn(b, lo, hi):
+            for j in range(lo, hi):
+                pairs = y_bf[:, j].bitcast(F32)
+                for u in range(2):
+                    at = (2 * (j - lo) + u) * P
+                    nc.tensor.transpose(bank[b][:, at : at + P], pairs[:, u * P : (u + 1) * P], ident[:])
+
+        def gather_words(b, lo, hi):
+            n = hi - lo
+            nc.scalar.copy(
+                out=y_grouped[:, lo:hi].bitcast(F32).rearrange("p j (m u) -> p j m u", u=2),
+                in_=bank[b][:, : n * 2 * P].rearrange("p (j u m) -> p j m u", u=2, m=P),
+            )
+
+        def quantize_y(lo, hi):
+            nc.vector.quantize_mx(
+                out=y_words[:, lo * P : hi * P].bitcast(E4M3),
+                scales=y_plane[:, lo * P : hi * P],
+                in_=y_grouped[:, lo:hi].rearrange("p j d -> p (j d)"),
+            )
+
+        def store_y(lo, hi):
+            nc.sync.dma_start(out=out_rows[:, lo:hi], in_=y[:, lo:hi])
+
+        def store_words(lo, hi):
+            nc.sync.dma_start(out=out_words[:, lo * P : hi * P], in_=y_words[:, lo * P : hi * P].bitcast(I32))
+
+        def store_scales(queues, lo, hi):
+            cols = slice(lo * P // 4, hi * P // 4)
+            for q in range(4):
+                queues[q].dma_start(
+                    out=out_scales[4 * q : 4 * q + 4, cols], in_=y_plane[32 * q : 32 * q + 4, :].bitcast(I32)[:, cols]
+                )
+
+        load_c(0)
+        nc.vector.memset(gain_rows[:], 0.0)
+        clear_plane(0, 0)
+        nc.vector.memset(lam_rows[:], 0.0)
+        clear_plane(1, 0)
+        nc.scalar.dma_start(out=logit_rows[:], in_=lam_logit.rearrange("h (a p) -> (h a) p", p=P))
+        nc.scalar.dma_start(out=gain_rows[:TILES, :], in_=gain.rearrange("h (a w) -> (h a) w", a=2))
+        make_identity(nc, ident[:])
+        nc.scalar.activation(out=lam_rows[:, 0:1], in_=lam_rows[:, 0:1], func=ACT.Sigmoid)
+        load_scales(0, 0)
+        load_words(0, 0, 0, HEAD_TILES)
+        load_words(1, 0, 0, HEAD_TILES)
+        load_c(1)
+        load_scales(1, 0)
+        load_words(0, 1, 0, HEAD_TILES)
+        load_c(2)
+        load_words(1, 1, 0, HEAD_TILES)
+        load_words(0, 2, 0, HEAD_TILES)
+        load_words(1, 2, 0, HEAD_TILES)
+        for run in (1, 2):
+            for a in range(2):
+                clear_plane(a, run)
+        for lo, hi in WORD_LOADS:
+            for run in (1, 2):
+                if SCALE_RUNS[run][0] == lo:
+                    load_scales(0, run)
+                    load_scales(1, run)
+            for a in range(2):
+                load_words(a, slice(0, PASSES), lo, hi)
+
+        nc.tensor.transpose(bank[0][:, :P], gain_rows[:].bitcast(F32), ident[:])
+        nc.scalar.activation(out=lam_rows[:TILES, :], in_=logit_rows[:], func=ACT.Sigmoid)
+        nc.scalar.copy(out=gain_cols[:], in_=bank[0][:, :TILES])
+        nc.tensor.transpose(bank[1][:, :P], lam_rows[:], ident[:])
+        nc.scalar.copy(out=lam[:], in_=bank[1][:, :TILES])
+
+        def spread_gain(b, pair):
+            for i in range(4):
+                col = gain_cols[:, 4 * pair + i : 4 * pair + i + 1]
+                nc.tensor.transpose(bank[b][:, i * P : (i + 1) * P], col.to_broadcast([P, P]), ident[:])
+
+        def keep_gain(b, pair):
+            nc.scalar.copy(out=gain_all[:].bitcast(F32)[:, pair * 512 : (pair + 1) * 512], in_=bank[b][:])
+
+        spread_gain(6, 0)
+        spread_gain(7, 1)
+
+        for g in range(PASSES):
+            interleave(nc.vector.tensor_copy, g, 0, D - SCALAR_COLS)
+            interleave(nc.scalar.copy, g, D - SCALAR_COLS, D)
+            quantize_c(g)
+            if g == 0:
+                keep_gain(6, 0)
+                keep_gain(7, 1)
+
+        for g in range(PASSES - 1):
+            for a in range(2):
+                for j in range(HEAD_TILES):
+                    product_pass(a, j, g)
+
+        whole = slice(0, D)
+        last = TILES - 1
+        for j in range(TILES):
+            todo = range(PASSES - 1, PASSES) if j < HEAD_TILES else range(PASSES)
+            for g in todo:
+                product_pass(0, j, g)
+            scale_second(j)
+            for g in todo:
+                product_pass(1, j, g)
+            if j > 0:
+                round_y(nc.scalar.copy, j - 1, 0, P)
+            if j == last:
+                break
+            subtract(j, whole)
+            if j % 4 == 2 and j > 2:
+                quantize_y(j - 6, j - 4)
+            if j % 4 == 3 and j > 3:
+                quantize_y(j - 5, j - 3)
+            apply_gain(j, whole)
+            if j == last - 1:
+                quantize_y(10, 12)
+            if j % 2 == 1:
+                store_y(j - 1, j + 1)
+            if j % 4 == 3 and j > 3:
+                store_words(j - 7, j - 3)
+            if j % 4 == 1 and j > 1:
+                turn(3, j - 5, j - 3)
+                turn(7, j - 3, j - 1)
+                if j < 13:
+                    spread_gain(2, (j + 3) // 4)
+                gather_words(3, j - 5, j - 3)
+                gather_words(7, j - 3, j - 1)
+                if j < 13:
+                    keep_gain(2, (j + 3) // 4)
+
+        store_y(last - 1, last)
+        store_words(8, 12)
+        store_scales([nc.sync] * 4, 0, 12)
+        halves = [slice(0, D // 2), slice(D // 2, D)]
+        turn(3, 12, 14)
+        gather_words(3, 12, 14)
+        turn(7, 14, 15)
+        gather_words(7, 14, 15)
+        for cols in halves:
+            subtract(last, cols)
+        for cols in halves:
+            apply_gain(last, cols)
+        store_y(last, TILES)
+        round_y(nc.vector.tensor_copy, last, 0, P // 2)
+        round_y(nc.vector.tensor_copy, last, P // 2, P)
+        turn(2, last, TILES)
+        gather_words(2, last, TILES)
+        quantize_y(12, 14)
+        quantize_y(14, 15)
+        store_words(12, 15)
+        quantize_y(last, TILES)
+        store_words(last, TILES)
+        store_scales([nc.sync, nc.sync, nc.scalar, nc.scalar], 12, TILES)

@@ -24,7 +24,6 @@ TILES = M // P
 HEAD_TILES = 4
 SCALAR_COLS = 160
 SCALE_RUNS = [(0, 4), (4, 8), (8, 16)]
-WORD_LOADS = [(4, 6), (6, 8), (8, 12), (12, 16)]
 
 
 def tile_differential_latent_read_k2_kernel(
@@ -68,7 +67,7 @@ def tile_differential_latent_read_k2_kernel(
 
         out_rows = out_0.rearrange("h (a p) d -> p (h a) d", p=P)
         out_words = out_1.rearrange("g p m t -> p (g m t)").bitcast(I32)
-        out_scales = out_2.rearrange("g q m -> q (g m)").bitcast(I32)
+        out_scales = out_2.rearrange("g (q r) m -> r q (g m)", r=4).bitcast(I32)
 
         def load_c(g):
             rows = c[g * P * PACK : (g + 1) * P * PACK, :]
@@ -88,7 +87,10 @@ def tile_differential_latent_read_k2_kernel(
             nc.vector.memset(a_plane[a][run][:].rearrange("p g n -> p (g n)").bitcast(I32), 0)
 
         def interleave(engine_copy, g, lo, hi):
-            engine_copy(out=c_grouped[:, g, lo:hi, :], in_=c_raw[:, g, :, lo:hi].rearrange("p j d -> p d j"))
+            engine_copy(
+                out=c_grouped[:, g, lo:hi, :].rearrange("p (d i) j -> p d j i", i=4),
+                in_=c_raw[:, g, :, lo:hi].rearrange("p j (d i) -> p d j i", i=4),
+            )
 
         def quantize_c(g):
             nc.vector.quantize_mx(
@@ -166,20 +168,22 @@ def tile_differential_latent_read_k2_kernel(
 
         def store_scales(queues, lo, hi):
             cols = slice(lo * P // 4, hi * P // 4)
-            for q in range(4):
-                queues[q].dma_start(
-                    out=out_scales[4 * q : 4 * q + 4, cols], in_=y_plane[32 * q : 32 * q + 4, :].bitcast(I32)[:, cols]
-                )
+            for r in range(4):
+                queues[r].dma_start(out=out_scales[r][:, cols], in_=y_plane[:].bitcast(I32)[r:P:32, cols])
 
+        every = slice(0, PASSES)
         load_c(0)
         nc.vector.memset(gain_rows[:], 0.0)
         clear_plane(0, 0)
         nc.vector.memset(lam_rows[:], 0.0)
         clear_plane(1, 0)
-        nc.scalar.dma_start(out=logit_rows[:], in_=lam_logit.rearrange("h (a p) -> (h a) p", p=P))
         nc.scalar.dma_start(out=gain_rows[:TILES, :], in_=gain.rearrange("h (a w) -> (h a) w", a=2))
         make_identity(nc, ident[:])
+        nc.gpsimd.dma_start(out=logit_rows[:], in_=lam_logit.rearrange("h (a p) -> (h a) p", p=P))
         nc.scalar.activation(out=lam_rows[:, 0:1], in_=lam_rows[:, 0:1], func=ACT.Sigmoid)
+        for run in (1, 2):
+            for a in range(2):
+                clear_plane(a, run)
         load_scales(0, 0)
         load_words(0, 0, 0, HEAD_TILES)
         load_words(1, 0, 0, HEAD_TILES)
@@ -188,24 +192,24 @@ def tile_differential_latent_read_k2_kernel(
         load_words(0, 1, 0, HEAD_TILES)
         load_c(2)
         load_words(1, 1, 0, HEAD_TILES)
+        load_scales(0, 1)
         load_words(0, 2, 0, HEAD_TILES)
         load_words(1, 2, 0, HEAD_TILES)
-        for run in (1, 2):
+        load_words(0, every, 4, 6)
+        load_scales(1, 1)
+        load_words(1, every, 4, 6)
+        load_scales(0, 2)
+        load_words(0, every, 6, 8)
+        load_words(1, every, 6, 8)
+        load_words(0, every, 8, 10)
+        load_scales(1, 2)
+        load_words(1, every, 8, 10)
+        for lo, hi in ((10, 12), (12, 16)):
             for a in range(2):
-                clear_plane(a, run)
-        for lo, hi in WORD_LOADS:
-            for run in (1, 2):
-                if SCALE_RUNS[run][0] == lo:
-                    load_scales(0, run)
-                    load_scales(1, run)
-            for a in range(2):
-                load_words(a, slice(0, PASSES), lo, hi)
+                load_words(a, every, lo, hi)
 
         nc.tensor.transpose(bank[0][:, :P], gain_rows[:].bitcast(F32), ident[:])
-        nc.scalar.activation(out=lam_rows[:TILES, :], in_=logit_rows[:], func=ACT.Sigmoid)
         nc.scalar.copy(out=gain_cols[:], in_=bank[0][:, :TILES])
-        nc.tensor.transpose(bank[1][:, :P], lam_rows[:], ident[:])
-        nc.scalar.copy(out=lam[:], in_=bank[1][:, :TILES])
 
         def spread_gain(b, pair):
             for i in range(4):
@@ -223,7 +227,10 @@ def tile_differential_latent_read_k2_kernel(
             interleave(nc.scalar.copy, g, D - SCALAR_COLS, D)
             quantize_c(g)
             if g == 0:
+                nc.scalar.activation(out=lam_rows[:TILES, :], in_=logit_rows[:], func=ACT.Sigmoid)
+                nc.tensor.transpose(bank[5][:, :P], lam_rows[:], ident[:])
                 keep_gain(6, 0)
+                nc.scalar.copy(out=lam[:], in_=bank[5][:, :TILES])
                 keep_gain(7, 1)
 
         for g in range(PASSES - 1):

@@ -23,6 +23,11 @@ PASSES = S // (P * PACK)
 TILES = M // P
 HEAD_TILES = 4
 SCALAR_COLS = 160
+GAIN_AT = {0: [], 1: [0], 2: [1], 3: [2], 4: [3], 5: [4], 6: [5, 6]}
+ROUND_AT = {0: [], 1: [], 2: [], 3: [0], 4: [1, 2], 5: [3], 6: [4], 7: [5, 6]}
+TURN_AT = {6: 0, 9: 4, 13: 8}
+SPREAD_AT = {4: 2, 10: 3}
+KEEP_AT = {6: 2, 10: 3}
 SCALE_RUNS = [(0, 4), (4, 8), (8, 16)]
 
 
@@ -32,7 +37,7 @@ def tile_differential_latent_read_k2_kernel(
     nc = tc.nc
     with ExitStack() as ctx:
         keep = ctx.enter_context(tc.tile_pool(name="keep", bufs=1))
-        work = ctx.enter_context(tc.tile_pool(name="work", bufs=4))
+        work = ctx.enter_context(tc.tile_pool(name="work", bufs=5))
         psum = ctx.enter_context(tc.psum_pool(name="psum", bufs=1))
         ctx.enter_context(tc.manual_schedule())
 
@@ -92,11 +97,11 @@ def tile_differential_latent_read_k2_kernel(
                 in_=c_raw[:, g, :, lo:hi].rearrange("p j (d i) -> p d j i", i=4),
             )
 
-        def quantize_c(g):
+        def quantize_c(g, lo, hi):
             nc.vector.quantize_mx(
-                out=c_words[:, g].bitcast(E4M3),
-                scales=c_plane[:, g],
-                in_=c_grouped[:, g].rearrange("p d j -> p (d j)"),
+                out=c_words[:, g, lo:hi].bitcast(E4M3),
+                scales=c_plane[:, g, lo:hi],
+                in_=c_grouped[:, g, lo:hi].rearrange("p d j -> p (d j)"),
             )
 
         def product_bank(a, j):
@@ -216,22 +221,24 @@ def tile_differential_latent_read_k2_kernel(
                 col = gain_cols[:, 4 * pair + i : 4 * pair + i + 1]
                 nc.tensor.transpose(bank[b][:, i * P : (i + 1) * P], col.to_broadcast([P, P]), ident[:])
 
-        def keep_gain(b, pair):
-            nc.scalar.copy(out=gain_all[:].bitcast(F32)[:, pair * 512 : (pair + 1) * 512], in_=bank[b][:])
+        def keep_gain(engine_copy, b, pair):
+            engine_copy(out=gain_all[:].bitcast(F32)[:, pair * 512 : (pair + 1) * 512], in_=bank[b][:])
 
         spread_gain(6, 0)
         spread_gain(7, 1)
 
         for g in range(PASSES):
-            interleave(nc.vector.tensor_copy, g, 0, D - SCALAR_COLS)
+            interleave(nc.vector.tensor_copy, g, 0, D // 2)
+            interleave(nc.vector.tensor_copy, g, D // 2, D - SCALAR_COLS)
             interleave(nc.scalar.copy, g, D - SCALAR_COLS, D)
-            quantize_c(g)
+            quantize_c(g, 0, D // 2)
+            quantize_c(g, D // 2, D)
             if g == 0:
                 nc.scalar.activation(out=lam_rows[:TILES, :], in_=logit_rows[:], func=ACT.Sigmoid)
                 nc.tensor.transpose(bank[5][:, :P], lam_rows[:], ident[:])
-                keep_gain(6, 0)
+                keep_gain(nc.scalar.copy, 6, 0)
                 nc.scalar.copy(out=lam[:], in_=bank[5][:, :TILES])
-                keep_gain(7, 1)
+                keep_gain(nc.scalar.copy, 7, 1)
 
         for g in range(PASSES - 1):
             for a in range(2):
@@ -247,31 +254,33 @@ def tile_differential_latent_read_k2_kernel(
             scale_second(j)
             for g in todo:
                 product_pass(1, j, g)
-            if j > 0:
-                round_y(nc.scalar.copy, j - 1, 0, P)
+            for i in ROUND_AT.get(j, [j - 1]):
+                round_y(nc.scalar.copy, i, 0, P)
             if j == last:
                 break
+            if j in SPREAD_AT:
+                spread_gain(2, SPREAD_AT[j])
+            if j in TURN_AT:
+                lo = TURN_AT[j]
+                turn(3, lo, lo + 2)
+                turn(7, lo + 2, lo + 4)
+                gather_words(3, lo, lo + 2)
+                gather_words(7, lo + 2, lo + 4)
             subtract(j, whole)
-            if j % 4 == 2 and j > 2:
-                quantize_y(j - 6, j - 4)
-            if j % 4 == 3 and j > 3:
-                quantize_y(j - 5, j - 3)
-            apply_gain(j, whole)
+            if j - 1 in TURN_AT:
+                quantize_y(TURN_AT[j - 1], TURN_AT[j - 1] + 2)
+            if j - 2 in TURN_AT:
+                quantize_y(TURN_AT[j - 2] + 2, TURN_AT[j - 2] + 4)
+            for i in GAIN_AT.get(j, [j]):
+                apply_gain(i, whole)
+                if i % 2 == 1:
+                    store_y(i - 1, i + 1)
+            if j in KEEP_AT:
+                keep_gain(nc.vector.tensor_copy, 2, KEEP_AT[j])
             if j == last - 1:
                 quantize_y(10, 12)
-            if j % 2 == 1:
-                store_y(j - 1, j + 1)
-            if j % 4 == 3 and j > 3:
-                store_words(j - 7, j - 3)
-            if j % 4 == 1 and j > 1:
-                turn(3, j - 5, j - 3)
-                turn(7, j - 3, j - 1)
-                if j < 13:
-                    spread_gain(2, (j + 3) // 4)
-                gather_words(3, j - 5, j - 3)
-                gather_words(7, j - 3, j - 1)
-                if j < 13:
-                    keep_gain(2, (j + 3) // 4)
+            if j - 2 in TURN_AT:
+                store_words(TURN_AT[j - 2], TURN_AT[j - 2] + 4)
 
         store_y(last - 1, last)
         store_words(8, 12)

@@ -26,8 +26,8 @@ SCALAR_COLS = 160
 GAIN_AT = {0: [], 1: [0], 2: [1], 3: [2], 4: [3], 5: [4], 6: [5, 6]}
 ROUND_AT = {0: [], 1: [], 2: [], 3: [0], 4: [1, 2], 5: [3], 6: [4], 7: [5, 6]}
 TURN_AT = {6: 0, 9: 4, 13: 8}
-SPREAD_AT = {4: 2, 10: 3}
-KEEP_AT = {6: 2, 10: 3}
+SPREAD_AT = {6: 2, 9: 3}
+KEEP_AT = {6: 2, 9: 3}
 SCALE_RUNS = [(0, 4), (4, 8), (8, 16)]
 
 
@@ -191,15 +191,15 @@ def tile_differential_latent_read_k2_kernel(
                 clear_plane(a, run)
         load_scales(0, 0)
         load_words(0, 0, 0, HEAD_TILES)
-        load_words(1, 0, 0, HEAD_TILES)
         load_c(1)
         load_scales(1, 0)
+        load_words(1, 0, 0, HEAD_TILES)
         load_words(0, 1, 0, HEAD_TILES)
         load_c(2)
         load_words(1, 1, 0, HEAD_TILES)
-        load_scales(0, 1)
         load_words(0, 2, 0, HEAD_TILES)
         load_words(1, 2, 0, HEAD_TILES)
+        load_scales(0, 1)
         load_words(0, every, 4, 6)
         load_scales(1, 1)
         load_words(1, every, 4, 6)
@@ -258,12 +258,12 @@ def tile_differential_latent_read_k2_kernel(
                 round_y(nc.scalar.copy, i, 0, P)
             if j == last:
                 break
-            if j in SPREAD_AT:
-                spread_gain(2, SPREAD_AT[j])
             if j in TURN_AT:
                 lo = TURN_AT[j]
                 turn(3, lo, lo + 2)
                 turn(7, lo + 2, lo + 4)
+                if j in SPREAD_AT:
+                    spread_gain(2, SPREAD_AT[j])
                 gather_words(3, lo, lo + 2)
                 gather_words(7, lo + 2, lo + 4)
             subtract(j, whole)
@@ -292,11 +292,17 @@ def tile_differential_latent_read_k2_kernel(
         gather_words(7, 14, 15)
         for cols in halves:
             subtract(last, cols)
-        for cols in halves:
-            apply_gain(last, cols)
+        by_pair = "m (p u e) -> m u p e"
+        last_gain = gain_all[:, (H - 1) * D :]
+        for lo, hi in ((0, P // 2), (P // 2, P)):
+            nc.vector.tensor_tensor(
+                out=y_bf[:, last].rearrange("m (u p e) -> m u p e", u=2, e=2)[:, :, lo:hi, :],
+                in0=diff[last][:].rearrange(by_pair, u=2, e=2)[:, :, lo:hi, :],
+                in1=last_gain.rearrange(by_pair, u=2, e=2)[:, :, lo:hi, :],
+                op=ALU.mult,
+            )
+        apply_gain(last, whole)
         store_y(last, TILES)
-        round_y(nc.vector.tensor_copy, last, 0, P // 2)
-        round_y(nc.vector.tensor_copy, last, P // 2, P)
         turn(2, last, TILES)
         gather_words(2, last, TILES)
         quantize_y(12, 14)

@@ -28,6 +28,7 @@ ROUND_AT = {0: [], 1: [], 2: [], 3: [0], 4: [1, 2], 5: [3], 6: [4], 7: [5, 6]}
 TURN_AT = {6: 0, 9: 4, 13: 8}
 SPREAD_AT = {6: 2, 9: 3}
 KEEP_AT = {6: 2, 9: 3}
+VECTOR_ROUNDS = (9, 12, 13)
 SCALE_RUNS = [(0, 4), (4, 8), (8, 16)]
 
 
@@ -45,18 +46,18 @@ def tile_differential_latent_read_k2_kernel(
 
         words_hbm = [w.rearrange("g p n t -> p g (n t)").bitcast(I32) for w in (a2_words, a1_words)]
         scales_hbm = [s.bitcast(I32).rearrange("g (q r) n -> r q g n", r=4) for s in (a2_scales, a1_scales)]
-        a_words = [keep.tile([P, PASSES, M], U32, name="a_words%d" % a, align_bytes=64) for a in range(2)]
+        def mx_operand(name, width, dtype, skip):
+            padded = keep.tile([P, skip + PASSES * width], dtype, name=name, align_bytes=256)
+            return padded[:, skip:].rearrange("p (g n) -> p g n", g=PASSES)
+
+        a_words = [mx_operand("a_words%d" % a, M, U32, 32) for a in range(2)]
         a_plane = [
-            [
-                keep.tile([P, PASSES, (hi - lo) * P], U8, name="a_plane%d_%d" % (a, lo), align_bytes=64)
-                for lo, hi in SCALE_RUNS
-            ]
-            for a in range(2)
+            [mx_operand("a_plane%d_%d" % (a, lo), (hi - lo) * P, U8, 192) for lo, hi in SCALE_RUNS] for a in range(2)
         ]
         c_raw = keep.tile([P, PASSES, PACK, D], BF16, align_bytes=64)
         c_grouped = keep.tile([P, PASSES, D, PACK], BF16, align_bytes=64)
-        c_words = keep.tile([P, PASSES, D], U32, align_bytes=64)
-        c_plane = keep.tile([P, PASSES, D], U8, align_bytes=64)
+        c_words = mx_operand("c_words", D, U32, 0)
+        c_plane = mx_operand("c_plane", D, U8, 64)
         ident = keep.tile([P, P], F32, align_bytes=64)
         gain_rows = keep.tile([P, 2 * P], BF16, align_bytes=64)
         gain_cols = keep.tile([P, TILES], F32, align_bytes=64)
@@ -183,8 +184,8 @@ def tile_differential_latent_read_k2_kernel(
         nc.vector.memset(lam_rows[:], 0.0)
         clear_plane(1, 0)
         nc.scalar.dma_start(out=gain_rows[:TILES, :], in_=gain.rearrange("h (a w) -> (h a) w", a=2))
-        make_identity(nc, ident[:])
         nc.gpsimd.dma_start(out=logit_rows[:], in_=lam_logit.rearrange("h (a p) -> (h a) p", p=P))
+        make_identity(nc, ident[:])
         nc.scalar.activation(out=lam_rows[:, 0:1], in_=lam_rows[:, 0:1], func=ACT.Sigmoid)
         for run in (1, 2):
             for a in range(2):
@@ -254,8 +255,9 @@ def tile_differential_latent_read_k2_kernel(
             scale_second(j)
             for g in todo:
                 product_pass(1, j, g)
-            for i in ROUND_AT.get(j, [j - 1]):
-                round_y(nc.scalar.copy, i, 0, P)
+            if j not in VECTOR_ROUNDS:
+                for i in ROUND_AT.get(j, [j - 1]):
+                    round_y(nc.scalar.copy, i, 0, P)
             if j == last:
                 break
             if j in TURN_AT:
@@ -267,6 +269,8 @@ def tile_differential_latent_read_k2_kernel(
                 gather_words(3, lo, lo + 2)
                 gather_words(7, lo + 2, lo + 4)
             subtract(j, whole)
+            if j in VECTOR_ROUNDS:
+                round_y(nc.vector.tensor_copy, j - 1, 0, P)
             if j - 1 in TURN_AT:
                 quantize_y(TURN_AT[j - 1], TURN_AT[j - 1] + 2)
             if j - 2 in TURN_AT:

from contextlib import ExitStack

import concourse.mybir as mybir
from concourse.masks import make_identity

H, T, S, D = 8, 256, 1536, 512
M = H * T
FLOPS = 2 * 2 * M * S * D

F32 = mybir.dt.float32
BF16 = mybir.dt.bfloat16
I32 = mybir.dt.int32
U32 = mybir.dt.uint32
U8 = mybir.dt.uint8
E4M3 = mybir.dt.float8_e4m3fn_x4
E5M2 = mybir.dt.float8_e5m2_x4
ACT = mybir.ActivationFunctionType
ALU = mybir.AluOpType

P = 128
PACK = 4
PASSES = S // (P * PACK)
TILES = M // P
HEAD_TILES = 4
SCALAR_COLS = 160
GAIN_AT = {0: [], 1: [0], 2: [1], 3: [2], 4: [3], 5: [4], 6: [5, 6]}
ROUND_AT = {0: [], 1: [], 2: [], 3: [0], 4: [1, 2], 5: [3], 6: [4], 7: [5, 6]}
TURN_AT = {6: 0, 9: 4, 13: 8}
SPREAD_AT = {6: 2, 9: 3}
KEEP_AT = {6: 2, 9: 3}
VECTOR_ROUNDS = (9, 12, 13)
SCALE_RUNS = [(0, 4), (4, 8), (8, 16)]


def tile_differential_latent_read_k2_kernel(
    tc, a1_words, a1_scales, a2_words, a2_scales, c, lam_logit, gain, out_0, out_1, out_2
):
    nc = tc.nc
    with ExitStack() as ctx:
        keep = ctx.enter_context(tc.tile_pool(name="keep", bufs=1))
        work = ctx.enter_context(tc.tile_pool(name="work", bufs=5))
        psum = ctx.enter_context(tc.psum_pool(name="psum", bufs=1))
        ctx.enter_context(tc.manual_schedule())

        bank = [psum.tile([P, 512], F32, name="bank%d" % b) for b in range(8)]

        words_hbm = [w.rearrange("g p n t -> p g (n t)").bitcast(I32) for w in (a2_words, a1_words)]
        scales_hbm = [s.bitcast(I32).rearrange("g (q r) n -> r q g n", r=4) for s in (a2_scales, a1_scales)]
        def mx_operand(name, width, dtype, skip):
            padded = keep.tile([P, skip + PASSES * width], dtype, name=name, align_bytes=256)
            return padded[:, skip:].rearrange("p (g n) -> p g n", g=PASSES)

        a_words = [mx_operand("a_words%d" % a, M, U32, 32) for a in range(2)]
        a_plane = [
            [mx_operand("a_plane%d_%d" % (a, lo), (hi - lo) * P, U8, 192) for lo, hi in SCALE_RUNS] for a in range(2)
        ]
        c_raw = keep.tile([P, PASSES, PACK, D], BF16, align_bytes=64)
        c_grouped = keep.tile([P, PASSES, D, PACK], BF16, align_bytes=64)
        c_words = mx_operand("c_words", D, U32, 0)
        c_plane = mx_operand("c_plane", D, U8, 64)
        ident = keep.tile([P, P], F32, align_bytes=64)
        gain_rows = keep.tile([P, 2 * P], BF16, align_bytes=64)
        gain_cols = keep.tile([P, TILES], F32, align_bytes=64)
        gain_all = keep.tile([P, H * D], BF16, align_bytes=64)
        logit_rows = keep.tile([TILES, P], BF16, align_bytes=64)
        lam_rows = keep.tile([P, P], F32, align_bytes=64)
        lam = keep.tile([P, TILES], F32, align_bytes=64)
        y = keep.tile([P, TILES, D], F32, align_bytes=64)
        y_bf = keep.tile([P, TILES, D], BF16, align_bytes=64)
        y_grouped = keep.tile([P, TILES, D], BF16, align_bytes=64)
        y_words = keep.tile([P, M], U32, align_bytes=64)
        y_plane = keep.tile([P, M], U8, align_bytes=64)

        out_rows = out_0.rearrange("h (a p) d -> p (h a) d", p=P)
        out_words = out_1.rearrange("g p m t -> p (g m t)").bitcast(I32)
        out_scales = out_2.rearrange("g (q r) m -> r q (g m)", r=4).bitcast(I32)

        def load_c(g):
            rows = c[g * P * PACK : (g + 1) * P * PACK, :]
            nc.sync.dma_start(out=c_raw[:, g], in_=rows.rearrange("(p j) d -> p j d", j=PACK))

        def load_scales(a, run):
            lo, hi = SCALE_RUNS[run]
            plane = a_plane[a][run][:].bitcast(I32)
            for r in range(4):
                nc.sync.dma_start(out=plane[r:P:32], in_=scales_hbm[a][r][:, :, lo * P // 4 : hi * P // 4])

        def load_words(a, passes, lo, hi):
            cols = slice(lo * P, hi * P)
            nc.sync.dma_start(out=a_words[a][:, passes, cols].bitcast(I32), in_=words_hbm[a][:, passes, cols])

        def clear_plane(a, run):
            nc.vector.memset(a_plane[a][run][:].rearrange("p g n -> p (g n)").bitcast(I32), 0)

        def interleave(engine_copy, g, lo, hi):
            engine_copy(
                out=c_grouped[:, g, lo:hi, :].rearrange("p (d i) j -> p d j i", i=4),
                in_=c_raw[:, g, :, lo:hi].rearrange("p j (d i) -> p d j i", i=4),
            )

        def quantize_c(g, lo, hi):
            nc.vector.quantize_mx(
                out=c_words[:, g, lo:hi].bitcast(E4M3),
                scales=c_plane[:, g, lo:hi],
                in_=c_grouped[:, g, lo:hi].rearrange("p d j -> p (d j)"),
            )

        def product_bank(a, j):
            return bank[4 * a + (j if j < HEAD_TILES else (j - HEAD_TILES) % (2 + a))]

        def product_pass(a, j, g):
            run = [r for r, (lo, hi) in enumerate(SCALE_RUNS) if lo <= j < hi][0]
            first = (j - SCALE_RUNS[run][0]) * P
            nc.tensor.matmul_mx(
                out=product_bank(a, j)[:],
                lhsT=a_words[a][:, g, j * P : (j + 1) * P].bitcast(E5M2),
                lhsT_scale=a_plane[a][run][:, g, first : first + P],
                rhs=c_words[:, g].bitcast(E4M3),
                rhs_scale=c_plane[:, g],
                start=(g == 0),
                stop=(g == PASSES - 1),
            )

        scaled = {}
        diff = {}

        def scale_second(j):
            scaled[j] = work.tile([P, D], F32, name="scaled")
            nc.scalar.activation(out=scaled[j][:], in_=product_bank(0, j)[:], func=ACT.Copy, scale=lam[:, j : j + 1])

        def subtract(j, cols):
            if j not in diff:
                diff[j] = work.tile([P, D], F32, name="diff")
            nc.vector.tensor_tensor(
                out=diff[j][:, cols], in0=product_bank(1, j)[:, cols], in1=scaled[j][:, cols], op=ALU.subtract
            )

        def apply_gain(j, cols):
            head_gain = gain_all[:, (j // 2) * D : (j // 2 + 1) * D]
            nc.vector.tensor_tensor(out=y[:, j, cols], in0=diff[j][:, cols], in1=head_gain[:, cols], op=ALU.mult)

        def round_y(engine_copy, j, lo, hi):
            engine_copy(
                out=y_bf[:, j].rearrange("m (u p e) -> m u p e", u=2, e=2)[:, :, lo:hi, :],
                in_=y[:, j].rearrange("m (p u e) -> m u p e", u=2, e=2)[:, :, lo:hi, :],
            )

        def turn(b, lo, hi):
            for j in range(lo, hi):
                pairs = y_bf[:, j].bitcast(F32)
                for u in range(2):
                    at = (2 * (j - lo) + u) * P
                    nc.tensor.transpose(bank[b][:, at : at + P], pairs[:, u * P : (u + 1) * P], ident[:])

        def gather_words(b, lo, hi):
            n = hi - lo
            nc.scalar.copy(
                out=y_grouped[:, lo:hi].bitcast(F32).rearrange("p j (m u) -> p j m u", u=2),
                in_=bank[b][:, : n * 2 * P].rearrange("p (j u m) -> p j m u", u=2, m=P),
            )

        def quantize_y(lo, hi):
            nc.vector.quantize_mx(
                out=y_words[:, lo * P : hi * P].bitcast(E4M3),
                scales=y_plane[:, lo * P : hi * P],
                in_=y_grouped[:, lo:hi].rearrange("p j d -> p (j d)"),
            )

        def store_y(lo, hi):
            nc.sync.dma_start(out=out_rows[:, lo:hi], in_=y[:, lo:hi])

        def store_words(lo, hi):
            nc.sync.dma_start(out=out_words[:, lo * P : hi * P], in_=y_words[:, lo * P : hi * P].bitcast(I32))

        def store_scales(queues, lo, hi):
            cols = slice(lo * P // 4, hi * P // 4)
            for r in range(4):
                queues[r].dma_start(out=out_scales[r][:, cols], in_=y_plane[:].bitcast(I32)[r:P:32, cols])

        every = slice(0, PASSES)
        load_c(0)
        nc.vector.memset(gain_rows[:], 0.0)
        clear_plane(0, 0)
        nc.vector.memset(lam_rows[:], 0.0)
        clear_plane(1, 0)
        nc.scalar.dma_start(out=gain_rows[:TILES, :], in_=gain.rearrange("h (a w) -> (h a) w", a=2))
        nc.gpsimd.dma_start(out=logit_rows[:], in_=lam_logit.rearrange("h (a p) -> (h a) p", p=P))
        make_identity(nc, ident[:])
        nc.scalar.activation(out=lam_rows[:, 0:1], in_=lam_rows[:, 0:1], func=ACT.Sigmoid)
        for run in (1, 2):
            for a in range(2):
                clear_plane(a, run)
        load_scales(0, 0)
        load_words(0, 0, 0, HEAD_TILES)
        load_c(1)
        load_scales(1, 0)
        load_words(1, 0, 0, HEAD_TILES)
        load_words(0, 1, 0, HEAD_TILES)
        load_c(2)
        load_words(1, 1, 0, HEAD_TILES)
        load_words(0, 2, 0, HEAD_TILES)
        load_words(1, 2, 0, HEAD_TILES)
        load_scales(0, 1)
        load_words(0, every, 4, 6)
        load_scales(1, 1)
        load_words(1, every, 4, 6)
        load_scales(0, 2)
        load_words(0, every, 6, 8)
        load_words(1, every, 6, 8)
        load_words(0, every, 8, 10)
        load_scales(1, 2)
        load_words(1, every, 8, 10)
        for lo, hi in ((10, 12), (12, 16)):
            for a in range(2):
                load_words(a, every, lo, hi)

        nc.tensor.transpose(bank[0][:, :P], gain_rows[:].bitcast(F32), ident[:])
        nc.scalar.copy(out=gain_cols[:], in_=bank[0][:, :TILES])

        def spread_gain(b, pair):
            for i in range(4):
                col = gain_cols[:, 4 * pair + i : 4 * pair + i + 1]
                nc.tensor.transpose(bank[b][:, i * P : (i + 1) * P], col.to_broadcast([P, P]), ident[:])

        def keep_gain(engine_copy, b, pair):
            engine_copy(out=gain_all[:].bitcast(F32)[:, pair * 512 : (pair + 1) * 512], in_=bank[b][:])

        spread_gain(6, 0)
        spread_gain(7, 1)

        for g in range(PASSES):
            interleave(nc.vector.tensor_copy, g, 0, D // 2)
            interleave(nc.vector.tensor_copy, g, D // 2, D - SCALAR_COLS)
            interleave(nc.scalar.copy, g, D - SCALAR_COLS, D)
            quantize_c(g, 0, D // 2)
            quantize_c(g, D // 2, D)
            if g == 0:
                nc.scalar.activation(out=lam_rows[:TILES, :], in_=logit_rows[:], func=ACT.Sigmoid)
                nc.tensor.transpose(bank[5][:, :P], lam_rows[:], ident[:])
                keep_gain(nc.scalar.copy, 6, 0)
                nc.scalar.copy(out=lam[:], in_=bank[5][:, :TILES])
                keep_gain(nc.scalar.copy, 7, 1)

        for g in range(PASSES - 1):
            for a in range(2):
                for j in range(HEAD_TILES):
                    product_pass(a, j, g)

        whole = slice(0, D)
        last = TILES - 1
        for j in range(TILES):
            todo = range(PASSES - 1, PASSES) if j < HEAD_TILES else range(PASSES)
            for g in todo:
                product_pass(0, j, g)
            scale_second(j)
            for g in todo:
                product_pass(1, j, g)
            if j not in VECTOR_ROUNDS:
                for i in ROUND_AT.get(j, [j - 1]):
                    round_y(nc.scalar.copy, i, 0, P)
            if j == last:
                break
            if j in TURN_AT:
                lo = TURN_AT[j]
                turn(3, lo, lo + 2)
                turn(7, lo + 2, lo + 4)
                if j in SPREAD_AT:
                    spread_gain(2, SPREAD_AT[j])
                gather_words(3, lo, lo + 2)
                gather_words(7, lo + 2, lo + 4)
            subtract(j, whole)
            if j in VECTOR_ROUNDS:
                round_y(nc.vector.tensor_copy, j - 1, 0, P)
            if j - 1 in TURN_AT:
                quantize_y(TURN_AT[j - 1], TURN_AT[j - 1] + 2)
            if j - 2 in TURN_AT:
                quantize_y(TURN_AT[j - 2] + 2, TURN_AT[j - 2] + 4)
            for i in GAIN_AT.get(j, [j]):
                apply_gain(i, whole)
                if i % 2 == 1:
                    store_y(i - 1, i + 1)
            if j in KEEP_AT:
                keep_gain(nc.vector.tensor_copy, 2, KEEP_AT[j])
            if j == last - 1:
                quantize_y(10, 12)
            if j - 2 in TURN_AT:
                store_words(TURN_AT[j - 2], TURN_AT[j - 2] + 4)

        store_y(last - 1, last)
        store_words(8, 12)
        store_scales([nc.sync] * 4, 0, 12)
        halves = [slice(0, D // 2), slice(D // 2, D)]
        turn(3, 12, 14)
        gather_words(3, 12, 14)
        turn(7, 14, 15)
        gather_words(7, 14, 15)
        for cols in halves:
            subtract(last, cols)
        by_pair = "m (p u e) -> m u p e"
        last_gain = gain_all[:, (H - 1) * D :]
        for lo, hi in ((0, P // 2), (P // 2, P)):
            nc.vector.tensor_tensor(
                out=y_bf[:, last].rearrange("m (u p e) -> m u p e", u=2, e=2)[:, :, lo:hi, :],
                in0=diff[last][:].rearrange(by_pair, u=2, e=2)[:, :, lo:hi, :],
                in1=last_gain.rearrange(by_pair, u=2, e=2)[:, :, lo:hi, :],
                op=ALU.mult,
            )
        apply_gain(last, whole)
        store_y(last, TILES)
        turn(2, last, TILES)
        gather_words(2, last, TILES)
        quantize_y(12, 14)
        quantize_y(14, 15)
        store_words(12, 15)
        quantize_y(last, TILES)
        store_words(last, TILES)
        store_scales([nc.sync, nc.sync, nc.scalar, nc.scalar], 12, TILES)
